import numpy as np
import ml_dtypes


def mxq(x, axis, fmt="e4m3"):
    dtype, down = {"e4m3": (ml_dtypes.float8_e4m3fn, 7), "e5m2": (ml_dtypes.float8_e5m2, 14)}[fmt]
    v = np.moveaxis(np.asarray(x, np.float32).astype(ml_dtypes.bfloat16).astype(np.float64), axis, -1)
    blocks = v.reshape(v.shape[:-1] + (-1, 32))
    amax = np.abs(blocks).max(-1, keepdims=True)
    byte = np.maximum(np.where(amax > 0, np.frexp(amax)[1] - 1 + 127, 0) - down, 1)
    scale = np.exp2(byte - 127.0)
    codes = (blocks / scale).astype(np.float32).astype(dtype).astype(np.float64)
    return np.moveaxis((codes * scale).reshape(v.shape), -1, axis)


WIDE = False


def mx_kscale(k):
    if not WIDE:
        return np.ones(k)
    levels = np.array([10, -10, 5, -5, 0])
    if k % 512:
        return np.exp2(np.random.permutation(np.resize(levels, k // 32))).repeat(32)
    a = np.empty((k // 512, 16))
    for p in range(k // 512):
        a[p, :8] = np.random.permutation(np.resize(levels, 8))
        for g in range(8):
            far = levels[np.abs(levels - a[p, g]) >= 10]
            a[p, g + 8] = far[np.random.randint(len(far))]
    return np.exp2(a.ravel()).repeat(32)


def f64(x):
    return np.asarray(x).astype(np.float64)


def striped(idx):
    return np.tile(idx.reshape(-1, 16).T, (8, 1)).astype(np.uint16)


def unstriped(offs):
    return offs[:16].T.reshape(-1).astype(np.int64)


def pack_weight(w):
    k, n = w.shape
    w = f64(np.asarray(w, np.float32).astype(ml_dtypes.bfloat16)).reshape(k // 32, 32, n)
    amax = np.abs(w).max(1)
    byte = np.clip(np.where(amax > 0, np.frexp(amax)[1] - 1 + 127 - 7, 1), 1, 254)
    scaled = (w * np.exp2(127.0 - byte)[:, None, :]).reshape(k, n).astype(np.float32)
    words = np.ascontiguousarray(scaled.reshape(k // 512, 128, 4, n).transpose(0, 1, 3, 2)).astype(ml_dtypes.float8_e4m3fn).view(np.uint8)
    return words, np.ascontiguousarray(byte.astype(np.uint8).reshape(k // 512, 16, n))


def unpack_weight(words, scales):
    g, p, n, _ = words.shape
    vals = np.ascontiguousarray(words).view(ml_dtypes.float8_e4m3fn).astype(np.float64) * np.repeat(np.exp2(scales.astype(np.float64) - 127.0), 8, axis=1)[..., None]
    return vals.transpose(0, 1, 3, 2).reshape(g * 512, n)


def planes(y):
    n, m = y.shape
    v = y.astype(np.float32).astype(ml_dtypes.bfloat16).astype(np.float64).reshape(n // 32, 32, m)
    top = np.abs(v).max(1)
    byte = np.clip(np.where(top > 0, np.frexp(top)[1] - 1 + 127 - 7, 1), 1, 254)
    codes = (v * np.exp2(127.0 - byte)[:, None, :]).reshape(n, m).astype(np.float32).astype(ml_dtypes.float8_e4m3fn).view(np.uint8)
    words = codes.reshape(n // 512, 128, 4, m).transpose(0, 1, 3, 2)
    return np.ascontiguousarray(words), np.ascontiguousarray(byte.astype(np.uint8).reshape(n // 512, 16, m))


def relu(v):
    return np.maximum(v, 0.0)


K, T, S, D, V, H, N = 512, 1024, 512, 3, 256, 512, 512
P = 2 ** 7


def setup_inputs():
    n = np.random.standard_normal
    s = mx_kscale(K)[:, None]
    u = mx_kscale(H)
    near = np.random.permutation(S)
    packed_xT = pack_weight(n((K, T)) * s)
    return {
        "x_words": packed_xT[0],
        "x_scales": packed_xT[1],
        "w1": (n((K, H)) / np.sqrt(K) / s * u).astype(np.float32),
        "w2": (n((H, N)) / np.sqrt(3 * H) / u[:, None]).astype(np.float32),
        "w3": (n((H, N)) / np.sqrt(3 * H) / u[:, None]).astype(np.float32),
        "w4": (n((H, N)) / np.sqrt(3 * H) / u[:, None]).astype(np.float32),
        "gate": (np.tile(np.random.uniform(0.2, 1.0, (D, 1, V)) / np.sqrt(D), (1, P, 1))).astype(np.float32),
        "gate2": (np.tile(np.random.uniform(0.2, 1.0, (D, 1, V)) / np.sqrt(D), (1, P, 1))).astype(np.float32),
        "offs": striped(np.random.permutation(T)[:S]),
        "cen": striped(np.random.permutation(S)[:V]),
        "pos1": striped(near[:V]),
        "pos2": striped(near[V:]),
        "pos3": striped(np.random.permutation(S)[:V]),
        "far1": striped(np.random.permutation(S)[:V]),
        "far2": striped(np.random.permutation(S)[:V]),
        "far3": striped(np.random.permutation(S)[:V]),
    }


def reference(x_words, x_scales, w1, w2, w3, w4, gate, gate2, offs, cen, pos1, pos2, pos3, far1, far2, far3):
    xq = unpack_weight(x_words, x_scales)[:, unstriped(offs)]
    h = relu(mxq(f64(w1), 0, "e4m3").T @ xq)
    z0 = h[:, unstriped(cen)]
    z1 = h[:, unstriped(pos1)] * f64(gate)[0, :1] + h[:, unstriped(pos2)] * f64(gate)[1, :1] + h[:, unstriped(pos3)] * f64(gate)[2, :1]
    z2 = h[:, unstriped(far1)] * f64(gate2)[0, :1] + h[:, unstriped(far2)] * f64(gate2)[1, :1] + h[:, unstriped(far3)] * f64(gate2)[2, :1]
    out_0 = relu(mxq(f64(w2), 0, "e4m3").T @ mxq(z0, 0, "e4m3") + mxq(f64(w3), 0, "e4m3").T @ mxq(z1, 0, "e4m3") + mxq(f64(w4), 0, "e4m3").T @ mxq(z2, 0, "e4m3"))
    return (out_0,) + planes(out_0)

@@ -1,0 +1,243 @@
+from contextlib import ExitStack
+
+import concourse.mybir as mybir
+from concourse.masks import make_identity
+
+K, T, S, D, V, H, N = 512, 1024, 512, 3, 256, 512, 512
+FLOPS = 2 * K * H * S + 3 * 2 * H * N * V
+
+F32 = mybir.dt.float32
+BF16 = mybir.dt.bfloat16
+I32 = mybir.dt.int32
+U32 = mybir.dt.uint32
+U16 = mybir.dt.uint16
+U8 = mybir.dt.uint8
+FP8X4 = mybir.dt.float8_e4m3fn_x4
+MULT = mybir.AluOpType.mult
+RELU = mybir.ActivationFunctionType.Relu
+COPY = mybir.ActivationFunctionType.Copy
+
+P = 128
+PACK = 4
+HALVES = V // P
+
+
+def tile_picked_zmix_relu_po_kernel(
+    tc, x_words, x_scales, w1, w2, w3, w4, gate, gate2, offs, cen, pos1, pos2, pos3, far1, far2, far3, out_0, out_1, out_2
+):
+    nc = tc.nc
+    with ExitStack() as ctx:
+        lists = ctx.enter_context(tc.tile_pool(name="lists", bufs=1))
+        sb = ctx.enter_context(tc.tile_pool(name="sb", bufs=1))
+        ps = ctx.enter_context(tc.psum_pool(name="ps", bufs=1))
+
+        def held(name, shape, dtype, tag=None):
+            return sb.tile(shape, dtype, name=name, tag=tag or name, align_bytes=64)
+
+        def bank(name, b, shape):
+            return ps.tile(shape, F32, name=name, tag="bank%d" % b)
+
+        def load_list(name, src):
+            t = lists.tile(list(src.shape), U16, name=name)
+            nc.sync.dma_start(t[:], src)
+            return t
+
+        def load_w(name, w, c0, c1):
+            t = held(name, [P, PACK, c1 - c0], F32)
+            nc.sync.dma_start(t[:], w[:, c0:c1].rearrange("(p j) c -> p j c", j=PACK))
+            return t
+
+        def load_gate(name, g):
+            t = held(name, [P, D, V], F32)
+            nc.sync.dma_start(t[:], g.rearrange("d p v -> p d v"))
+            return t
+
+        def quantize(name, src, width, tag=None):
+            codes = held(name + "_codes", [P, width], U32, tag)
+            scales = held(name + "_scales", [P, width], U8)
+            nc.vector.quantize_mx(out=codes[:].bitcast(FP8X4), scales=scales[:], in_=src)
+            return codes, scales
+
+        def mx(out, stat, scols, mov, mcols, start, stop):
+            nc.tensor.matmul_mx(
+                out=out,
+                lhsT=stat[0][:, scols].bitcast(FP8X4),
+                lhsT_scale=stat[1][:, scols],
+                rhs=mov[0][:, mcols].bitcast(FP8X4),
+                rhs_scale=mov[1][:, mcols],
+                start=start,
+                stop=stop,
+            )
+
+        xs = held("xs", [P, T], U8)
+        nc.gpsimd.memset(xs[:].bitcast(I32), 0)
+        offs_t = load_list("offs_t", offs)
+        for q in range(4):
+            nc.sync.dma_start(xs[32 * q : 32 * q + 4, :].bitcast(I32), x_scales[0, 4 * q : 4 * q + 4, :].bitcast(I32))
+        xw = held("xw", [P, T], U32)
+        nc.sync.dma_start(xw[:].bitcast(I32), x_words[0].rearrange("p n t -> p (n t)").bitcast(I32))
+        w1_raw = [load_w("w1r0", w1, 0, P), load_w("w1r1", w1, P, 2 * P)]
+        gate_t = load_gate("gate_t", gate)
+        cen_t = load_list("cen_t", cen)
+        pos_t = [load_list("pos1_t", pos1)]
+        w1_rest = load_w("w1r2", w1, 2 * P, 4 * P)
+        pos_t.append(load_list("pos2_t", pos2))
+        pos_t.append(load_list("pos3_t", pos3))
+        w2_raw = load_w("w2r", w2, 0, N)
+        w3_raw = load_w("w3r", w3, 0, N)
+        w4_raw = load_w("w4r", w4, 0, N)
+        gate2_t = load_gate("gate2_t", gate2)
+        far_t = [load_list("far1_t", far1), load_list("far2_t", far2), load_list("far3_t", far3)]
+
+        ident = held("ident", [P, P], F32)
+        make_identity(nc, ident[:])
+
+        w1_src = [w1_raw[0][:], w1_raw[1][:], w1_rest[:, :, 0:P], w1_rest[:, :, P : 2 * P]]
+
+        def w1_quantized(c):
+            b = held("w1b%d" % c, [P, P * PACK], BF16)
+            nc.scalar.activation(
+                b[:].rearrange("p (a i j) -> p a j i", i=4, j=PACK),
+                w1_src[c].rearrange("p j (a i) -> p a j i", i=4),
+                COPY,
+            )
+            return quantize("w1q%d" % c, b[:], P)
+
+        xs_g = held("xs_g", [P, S], U8)
+        nc.vector.tensor_copy(xs_g[:], xs[:].indirect(offs_t[:]))
+        w1q = [w1_quantized(0)]
+        xw_g = held("xw_g", [P, S], U32)
+        h = [held("h%d" % c, [P, S], F32) for c in range(4)]
+        for a in range(2):
+            cols = slice(a * 256, (a + 1) * 256)
+            nc.vector.tensor_copy(xw_g[:, cols], xw[:].indirect(offs_t[:, 16 * a : 16 * (a + 1)]))
+            acc = bank("h0acc%d" % a, a, [P, 256])
+            mx(acc[:], w1q[0], slice(0, P), (xw_g, xs_g), cols, True, True)
+            nc.scalar.activation(h[0][:, cols], acc[:], RELU)
+
+        def make_h(c):
+            w1q.append(w1_quantized(c))
+            acc = bank("hacc%d" % c, (c + 1) % 4, [P, S])
+            mx(acc[:], w1q[c], slice(0, P), (xw_g, xs_g), slice(0, S), True, True)
+            nc.scalar.activation(h[c][:], acc[:], RELU)
+
+        def cast_w(name, raw, tag=None):
+            b = held(name, [P, N * PACK], BF16)
+            for c in range(4):
+                nc.scalar.copy(
+                    b[:].rearrange("p (t m j) -> p m j t", t=PACK, j=PACK)[:, 32 * c : 32 * (c + 1)],
+                    raw[:].rearrange("p j (m t) -> p m j t", t=PACK)[:, 32 * c : 32 * (c + 1)],
+                )
+            return b
+
+        def turn_forward(fwd, c, terms):
+            for d, term in enumerate(terms):
+                for acc, cols in fwd:
+                    nc.tensor.matmul(
+                        acc[:, c * P : (c + 1) * P], term[:, cols], ident[:], start=(d == 0), stop=(d == len(terms) - 1), is_transpose=True
+                    )
+
+        def round_chunks(eng, zt, acc, c0, c1):
+            eng(
+                zt[:].rearrange("v (u p e) -> v u p e", u=2, e=2)[:, :, 32 * c0 : 32 * c1, :],
+                acc[:].rearrange("v (p u e) -> v u p e", u=2, e=2)[:, :, 32 * c0 : 32 * c1, :],
+            )
+
+        def turn_back(zt, back):
+            for u in range(2):
+                nc.tensor.transpose(back[:, u, :], zt[:].bitcast(F32)[:, u * P : (u + 1) * P], ident[:])
+
+        halves = [slice(a * P, (a + 1) * P) for a in range(HALVES)]
+
+        def gather(name, c, lst, g, d, cols, tag=None):
+            n = cols.stop - cols.start
+            t = held(name, [P, n], F32, tag)
+            win = h[c][:].indirect(lst[:, cols.start // 16 : cols.stop // 16])
+            if g is None:
+                nc.vector.tensor_copy(t[:], win)
+            else:
+                nc.vector.tensor_tensor(t[:], win, g[:, d, cols], MULT)
+            return t
+
+        z0_fwd = [(bank("z0f%d" % a, 4 + a, [P, H]), halves[a]) for a in range(HALVES)]
+        z1_fwd = [(bank("z1f%d" % a, 6 + a, [P, H]), halves[a]) for a in range(HALVES)]
+        whole = slice(0, V)
+        wq = {}
+        for c in range(4):
+            if c + 1 < 4:
+                make_h(c + 1)
+            turn_forward(z0_fwd, c, [gather("own%d" % c, c, cen_t, None, 0, whole)])
+            turn_forward(z1_fwd, c, [gather("near%d_%d" % (c, d), c, pos_t[d], gate_t, d, whole) for d in range(D)])
+        wb = [cast_w("w2b", w2_raw), cast_w("w3b", w3_raw), cast_w("w4b", w4_raw)]
+
+        def finish_z(name, fwd, back_bank):
+            back = bank(name + "back", back_bank, [P, HALVES, 2, P])
+            for a in range(HALVES):
+                zt = held(name + "t%d" % a, [P, H], BF16)
+                round_chunks(nc.scalar.copy, zt, fwd[a][0], 0, 4)
+                turn_back(zt, back[:, a])
+            zb = held(name + "b", [P, V * PACK], BF16)
+            nc.scalar.copy(
+                zb[:].bitcast(F32).rearrange("p (a v u) -> p a v u", a=HALVES, u=2),
+                back[:].rearrange("p a u v -> p a v u"),
+            )
+            return zb
+
+        z0b = finish_z("z0", z0_fwd, 1)
+        z1b = finish_z("z1", z1_fwd, 2)
+
+        z2_fwd = [(bank("z2f%d" % a, 4 + a, [P, H]), halves[a]) for a in range(HALVES)]
+        z2t = [held("z2t%d" % a, [P, H], BF16) for a in range(HALVES)]
+        acc = [bank("out%d" % t, b, [P, V]) for t, b in enumerate((0, 3, 6, 7))]
+        for c in range(4):
+            tag = None
+            if c == 1:
+                wq[0] = quantize("w2q", wb[0][:], N)
+                tag = "w2b"
+            if c == 3:
+                z0q = quantize("z0q", z0b[:], V)
+                tag = "z0b"
+                for t in range(PACK):
+                    mx(acc[t][:], wq[0], slice(t * P, (t + 1) * P), z0q, whole, True, False)
+            last = [gather("far%d_%d" % (c, d), c, far_t[d], gate2_t, d, whole, tag if d == 0 else None) for d in range(D)]
+            turn_forward(z2_fwd, c, last)
+            if c == 2:
+                for a in range(HALVES):
+                    round_chunks(nc.scalar.copy, z2t[a], z2_fwd[a][0], 0, 3)
+        wq[2] = quantize("w4q", wb[2][:], N, "gate2_t")
+        wq[1] = quantize("w3q", wb[1][:], N, "h3")
+        z1q = quantize("z1q", z1b[:], V, "w4b")
+
+        z2b = held("z2b", [P, V * PACK], BF16)
+        backs = []
+        for a in range(HALVES):
+            round_chunks(nc.scalar.copy, z2t[a], z2_fwd[a][0], 3, 4)
+            backs.append(bank("z2back%d" % a, 1 + a, [P, 2, P]))
+            turn_back(z2t[a], backs[a])
+        for a in range(HALVES):
+            nc.scalar.copy(
+                z2b[:].bitcast(F32).rearrange("p (a v u) -> p a v u", a=HALVES, u=2)[:, a],
+                backs[a][:].rearrange("p u v -> p v u"),
+            )
+        for t in range(PACK):
+            mx(acc[t][:], wq[1], slice(t * P, (t + 1) * P), z1q, whole, False, False)
+        z2q = quantize("z2q", z2b[:], V)
+
+        y = held("y", [P, PACK, V], F32)
+        out_rows = out_0.rearrange("(p t) v -> p t v", t=PACK)
+        for t in range(PACK):
+            mx(acc[t][:], wq[2], slice(t * P, (t + 1) * P), z2q, whole, False, True)
+            if t % 2 == 0:
+                nc.scalar.activation(y[:, t, :], acc[t][:], RELU)
+            else:
+                nc.vector.tensor_scalar_max(y[:, t, :], acc[t][:], 0.0)
+        nc.sync.dma_start(out_rows, y[:])
+        yb = held("yb", [P, V * PACK], BF16)
+        nc.vector.tensor_copy(
+            yb[:].rearrange("p (a i t) -> p a t i", i=4, t=PACK), y[:].rearrange("p t (a i) -> p a t i", i=4)
+        )
+        y_codes, y_scales = quantize("yq", yb[:], V)
+        nc.sync.dma_start(out_1[0].rearrange("p n t -> p (n t)").bitcast(I32), y_codes[:].bitcast(I32))
+        for q in range(4):
+            eng = nc.scalar if q % 2 else nc.sync
+            eng.dma_start(out_2[0, 4 * q : 4 * q + 4, :].bitcast(I32), y_scales[32 * q : 32 * q + 4, :].bitcast(I32))

@@ -72,11 +72,12 @@ def tile_picked_zmix_relu_po_kernel(
         xs = held("xs", [P, T], U8)
         nc.gpsimd.memset(xs[:].bitcast(I32), 0)
         offs_t = load_list("offs_t", offs)
+        w1_raw = [load_w("w1r0", w1, 0, P)]
         for q in range(4):
             nc.sync.dma_start(xs[32 * q : 32 * q + 4, :].bitcast(I32), x_scales[0, 4 * q : 4 * q + 4, :].bitcast(I32))
         xw = held("xw", [P, T], U32)
         nc.sync.dma_start(xw[:].bitcast(I32), x_words[0].rearrange("p n t -> p (n t)").bitcast(I32))
-        w1_raw = [load_w("w1r0", w1, 0, P), load_w("w1r1", w1, P, 2 * P)]
+        w1_raw.append(load_w("w1r1", w1, P, 2 * P))
         gate_t = load_gate("gate_t", gate)
         cen_t = load_list("cen_t", cen)
         pos_t = [load_list("pos1_t", pos1)]
@@ -109,11 +110,12 @@ def tile_picked_zmix_relu_po_kernel(
         xw_g = held("xw_g", [P, S], U32)
         h = [held("h%d" % c, [P, S], F32) for c in range(4)]
         for a in range(2):
+            nc.vector.tensor_copy(xw_g[:, a * 256 : (a + 1) * 256], xw[:].indirect(offs_t[:, 16 * a : 16 * (a + 1)]))
+        for a in range(2):
             cols = slice(a * 256, (a + 1) * 256)
-            nc.vector.tensor_copy(xw_g[:, cols], xw[:].indirect(offs_t[:, 16 * a : 16 * (a + 1)]))
             acc = bank("h0acc%d" % a, a, [P, 256])
             mx(acc[:], w1q[0], slice(0, P), (xw_g, xs_g), cols, True, True)
-            nc.scalar.activation(h[0][:, cols], acc[:], RELU)
+            nc.vector.tensor_scalar_max(h[0][:, cols], acc[:], 0.0)
 
         def make_h(c):
             w1q.append(w1_quantized(c))
@@ -123,10 +125,10 @@ def tile_picked_zmix_relu_po_kernel(
 
         def cast_w(name, raw, tag=None):
             b = held(name, [P, N * PACK], BF16)
-            for c in range(4):
+            for c in range(2):
                 nc.scalar.copy(
-                    b[:].rearrange("p (t m j) -> p m j t", t=PACK, j=PACK)[:, 32 * c : 32 * (c + 1)],
-                    raw[:].rearrange("p j (m t) -> p m j t", t=PACK)[:, 32 * c : 32 * (c + 1)],
+                    b[:].rearrange("p (t m j) -> p m j t", t=PACK, j=PACK)[:, 64 * c : 64 * (c + 1)],
+                    raw[:].rearrange("p j (m t) -> p m j t", t=PACK)[:, 64 * c : 64 * (c + 1)],
                 )
             return b
 
@@ -189,39 +191,34 @@ def tile_picked_zmix_relu_po_kernel(
         z2_fwd = [(bank("z2f%d" % a, 4 + a, [P, H]), halves[a]) for a in range(HALVES)]
         z2t = [held("z2t%d" % a, [P, H], BF16) for a in range(HALVES)]
         acc = [bank("out%d" % t, b, [P, V]) for t, b in enumerate((0, 3, 6, 7))]
-        for c in range(4):
-            tag = None
-            if c == 1:
-                wq[0] = quantize("w2q", wb[0][:], N)
-                tag = "w2b"
-            if c == 3:
-                z0q = quantize("z0q", z0b[:], V)
-                tag = "z0b"
-                for t in range(PACK):
-                    mx(acc[t][:], wq[0], slice(t * P, (t + 1) * P), z0q, whole, True, False)
-            last = [gather("far%d_%d" % (c, d), c, far_t[d], gate2_t, d, whole, tag if d == 0 else None) for d in range(D)]
-            turn_forward(z2_fwd, c, last)
-            if c == 2:
-                for a in range(HALVES):
-                    round_chunks(nc.scalar.copy, z2t[a], z2_fwd[a][0], 0, 3)
-        wq[2] = quantize("w4q", wb[2][:], N, "gate2_t")
-        wq[1] = quantize("w3q", wb[1][:], N, "h3")
-        z1q = quantize("z1q", z1b[:], V, "w4b")
-
-        z2b = held("z2b", [P, V * PACK], BF16)
-        backs = []
+        for c in range(3):
+            turn_forward(z2_fwd, c, [gather("far%d_%d" % (c, d), c, far_t[d], gate2_t, d, whole) for d in range(D)])
         for a in range(HALVES):
+            round_chunks(nc.scalar.copy, z2t[a], z2_fwd[a][0], 0, 3)
+        wq[0] = quantize("w2q", wb[0][:], N)
+        z0q = quantize("z0q", z0b[:], V)
+        for t in range(PACK):
+            mx(acc[t][:], wq[0], slice(t * P, (t + 1) * P), z0q, whole, True, False)
+        z2_codes = held("z2_codes", [P, V], U32)
+        z2_scales = held("z2_scales", [P, V], U8)
+        z2q = (z2_codes, z2_scales)
+        z2b = []
+        for a in range(HALVES):
+            tags = ["z0b", "late1", "late2"] if a == 0 else [None] * D
+            last = [gather("far3_%d_%d" % (d, a), 3, far_t[d], gate2_t, d, halves[a], tags[d]) for d in range(D)]
+            turn_forward([(z2_fwd[a][0], slice(0, P))], 3, last)
             round_chunks(nc.scalar.copy, z2t[a], z2_fwd[a][0], 3, 4)
-            backs.append(bank("z2back%d" % a, 1 + a, [P, 2, P]))
-            turn_back(z2t[a], backs[a])
-        for a in range(HALVES):
-            nc.scalar.copy(
-                z2b[:].bitcast(F32).rearrange("p (a v u) -> p a v u", a=HALVES, u=2)[:, a],
-                backs[a][:].rearrange("p u v -> p v u"),
-            )
+            back = bank("z2back%d" % a, 1 + a, [P, 2, P])
+            turn_back(z2t[a], back)
+            z2b.append(held("z2b%d" % a, [P, P * PACK], BF16))
+            nc.scalar.copy(z2b[a][:].bitcast(F32).rearrange("p (v u) -> p v u", u=2), back[:].rearrange("p u v -> p v u"))
+        wq[1] = quantize("w3q", wb[1][:], N, "z0b")
+        z1q = quantize("z1q", z1b[:], V, "late1")
         for t in range(PACK):
             mx(acc[t][:], wq[1], slice(t * P, (t + 1) * P), z1q, whole, False, False)
-        z2q = quantize("z2q", z2b[:], V)
+        wq[2] = quantize("w4q", wb[2][:], N, "late2")
+        for a in range(HALVES):
+            nc.vector.quantize_mx(out=z2_codes[:, halves[a]].bitcast(FP8X4), scales=z2_scales[:, halves[a]], in_=z2b[a][:])
 
         y = held("y", [P, PACK, V], F32)
         out_rows = out_0.rearrange("(p t) v -> p t v", t=PACK)
@@ -231,11 +228,13 @@ def tile_picked_zmix_relu_po_kernel(
                 nc.scalar.activation(y[:, t, :], acc[t][:], RELU)
             else:
                 nc.vector.tensor_scalar_max(y[:, t, :], acc[t][:], 0.0)
-        nc.sync.dma_start(out_rows, y[:])
+                nc.sync.dma_start(out_rows[:, t - 1 : t + 1, :], y[:, t - 1 : t + 1, :])
         yb = held("yb", [P, V * PACK], BF16)
-        nc.vector.tensor_copy(
-            yb[:].rearrange("p (a i t) -> p a t i", i=4, t=PACK), y[:].rearrange("p t (a i) -> p a t i", i=4)
-        )
+        for eng, quads in ((nc.vector.tensor_copy, slice(0, 44)), (nc.scalar.copy, slice(44, 64))):
+            eng(
+                yb[:].rearrange("p (a i t) -> p a t i", i=4, t=PACK)[:, quads],
+                y[:].rearrange("p t (a i) -> p a t i", i=4)[:, quads],
+            )
         y_codes, y_scales = quantize("yq", yb[:], V)
         nc.sync.dma_start(out_1[0].rearrange("p n t -> p (n t)").bitcast(I32), y_codes[:].bitcast(I32))
         for q in range(4):

@@ -47,8 +47,8 @@ def tile_picked_zmix_relu_po_kernel(
             nc.sync.dma_start(t[:], w[:, c0:c1].rearrange("(p j) c -> p j c", j=PACK))
             return t
 
-        def load_gate(name, g):
-            t = held(name, [P, D, V], F32)
+        def load_gate(name, g, tag=None):
+            t = held(name, [P, D, V], F32, tag)
             nc.sync.dma_start(t[:], g.rearrange("d p v -> p d v"))
             return t
 
@@ -78,16 +78,15 @@ def tile_picked_zmix_relu_po_kernel(
         xw = held("xw", [P, T], U32)
         nc.sync.dma_start(xw[:].bitcast(I32), x_words[0].rearrange("p n t -> p (n t)").bitcast(I32))
         w1_raw.append(load_w("w1r1", w1, P, 2 * P))
-        gate_t = load_gate("gate_t", gate)
-        cen_t = load_list("cen_t", cen)
-        pos_t = [load_list("pos1_t", pos1)]
         w1_rest = load_w("w1r2", w1, 2 * P, 4 * P)
+        cen_t = load_list("cen_t", cen)
+        gate_t = load_gate("gate_t", gate)
+        pos_t = [load_list("pos1_t", pos1)]
         pos_t.append(load_list("pos2_t", pos2))
         pos_t.append(load_list("pos3_t", pos3))
         w2_raw = load_w("w2r", w2, 0, N)
         w3_raw = load_w("w3r", w3, 0, N)
         w4_raw = load_w("w4r", w4, 0, N)
-        gate2_t = load_gate("gate2_t", gate2)
         far_t = [load_list("far1_t", far1), load_list("far2_t", far2), load_list("far3_t", far3)]
 
         ident = held("ident", [P, P], F32)
@@ -95,20 +94,20 @@ def tile_picked_zmix_relu_po_kernel(
 
         w1_src = [w1_raw[0][:], w1_raw[1][:], w1_rest[:, :, 0:P], w1_rest[:, :, P : 2 * P]]
 
-        def w1_quantized(c):
+        def w1_cast(c):
             b = held("w1b%d" % c, [P, P * PACK], BF16)
             nc.scalar.activation(
                 b[:].rearrange("p (a i j) -> p a j i", i=4, j=PACK),
                 w1_src[c].rearrange("p j (a i) -> p a j i", i=4),
                 COPY,
             )
-            return quantize("w1q%d" % c, b[:], P)
+            return b
 
         xs_g = held("xs_g", [P, S], U8)
         nc.vector.tensor_copy(xs_g[:], xs[:].indirect(offs_t[:]))
-        w1q = [w1_quantized(0)]
+        w1q = [quantize("w1q0", w1_cast(0)[:], P)]
         xw_g = held("xw_g", [P, S], U32)
-        h = [held("h%d" % c, [P, S], F32) for c in range(4)]
+        h = [held("h0", [P, S], F32)]
         for a in range(2):
             nc.vector.tensor_copy(xw_g[:, a * 256 : (a + 1) * 256], xw[:].indirect(offs_t[:, 16 * a : 16 * (a + 1)]))
         for a in range(2):
@@ -117,11 +116,15 @@ def tile_picked_zmix_relu_po_kernel(
             mx(acc[:], w1q[0], slice(0, P), (xw_g, xs_g), cols, True, True)
             nc.vector.tensor_scalar_max(h[0][:, cols], acc[:], 0.0)
 
-        def make_h(c):
-            w1q.append(w1_quantized(c))
+        w1b = [w1_cast(c) for c in range(1, 4)]
+        for c in range(1, 4):
+            w1q.append(quantize("w1q%d" % c, w1b[c - 1][:], P))
+            h.append(held("h%d" % c, [P, S], F32, "w1r2" if c == 1 else None))
             acc = bank("hacc%d" % c, (c + 1) % 4, [P, S])
             mx(acc[:], w1q[c], slice(0, P), (xw_g, xs_g), slice(0, S), True, True)
             nc.scalar.activation(h[c][:], acc[:], RELU)
+
+        gate2_t = load_gate("gate2_t", gate2, "w1q3_codes")
 
         def cast_w(name, raw, tag=None):
             b = held(name, [P, N * PACK], BF16)
@@ -141,13 +144,13 @@ def tile_picked_zmix_relu_po_kernel(
 
         def round_chunks(eng, zt, acc, c0, c1):
             eng(
-                zt[:].rearrange("v (u p e) -> v u p e", u=2, e=2)[:, :, 32 * c0 : 32 * c1, :],
+                zt.rearrange("v (u p e) -> v u p e", u=2, e=2)[:, :, 32 * c0 : 32 * c1, :],
                 acc[:].rearrange("v (p u e) -> v u p e", u=2, e=2)[:, :, 32 * c0 : 32 * c1, :],
             )
 
         def turn_back(zt, back):
             for u in range(2):
-                nc.tensor.transpose(back[:, u, :], zt[:].bitcast(F32)[:, u * P : (u + 1) * P], ident[:])
+                nc.tensor.transpose(back[:, u, :], zt.bitcast(F32)[:, u * P : (u + 1) * P], ident[:])
 
         halves = [slice(a * P, (a + 1) * P) for a in range(HALVES)]
 
@@ -166,37 +169,37 @@ def tile_picked_zmix_relu_po_kernel(
         whole = slice(0, V)
         wq = {}
         for c in range(4):
-            if c + 1 < 4:
-                make_h(c + 1)
             turn_forward(z0_fwd, c, [gather("own%d" % c, c, cen_t, None, 0, whole)])
             turn_forward(z1_fwd, c, [gather("near%d_%d" % (c, d), c, pos_t[d], gate_t, d, whole) for d in range(D)])
         wb = [cast_w("w2b", w2_raw), cast_w("w3b", w3_raw), cast_w("w4b", w4_raw)]
 
-        def finish_z(name, fwd, back_bank):
-            back = bank(name + "back", back_bank, [P, HALVES, 2, P])
+        zt_all = held("zt_all", [P, 2 * HALVES * H], BF16, "w4r")
+
+        def finish_z(name, fwd, backs, first):
             for a in range(HALVES):
-                zt = held(name + "t%d" % a, [P, H], BF16)
+                zt = zt_all[:, (first + a) * H : (first + a + 1) * H]
                 round_chunks(nc.scalar.copy, zt, fwd[a][0], 0, 4)
-                turn_back(zt, back[:, a])
+                turn_back(zt, backs[a])
             zb = held(name + "b", [P, V * PACK], BF16)
-            nc.scalar.copy(
-                zb[:].bitcast(F32).rearrange("p (a v u) -> p a v u", a=HALVES, u=2),
-                back[:].rearrange("p a u v -> p a v u"),
-            )
+            for a in range(HALVES):
+                nc.scalar.copy(
+                    zb[:].bitcast(F32).rearrange("p (a v u) -> p a v u", a=HALVES, u=2)[:, a],
+                    backs[a][:].rearrange("p u v -> p v u"),
+                )
             return zb
 
-        z0b = finish_z("z0", z0_fwd, 1)
-        z1b = finish_z("z1", z1_fwd, 2)
+        z0b = finish_z("z0", z0_fwd, [bank("z0back%d" % a, 1 + a, [P, 2, P]) for a in range(HALVES)], 0)
+        z1b = finish_z("z1", z1_fwd, [bank("z1back%d" % a, 4 + a, [P, 2, P]) for a in range(HALVES)], HALVES)
 
         z2_fwd = [(bank("z2f%d" % a, 4 + a, [P, H]), halves[a]) for a in range(HALVES)]
-        z2t = [held("z2t%d" % a, [P, H], BF16) for a in range(HALVES)]
+        z2t = [held("z2t%d" % a, [P, H], BF16)[:] for a in range(HALVES)]
         acc = [bank("out%d" % t, b, [P, V]) for t, b in enumerate((0, 3, 6, 7))]
         for c in range(3):
             turn_forward(z2_fwd, c, [gather("far%d_%d" % (c, d), c, far_t[d], gate2_t, d, whole) for d in range(D)])
         for a in range(HALVES):
             round_chunks(nc.scalar.copy, z2t[a], z2_fwd[a][0], 0, 3)
         wq[0] = quantize("w2q", wb[0][:], N)
-        z0q = quantize("z0q", z0b[:], V)
+        z0q = quantize("z0q", z0b[:], V, "far0_0")
         for t in range(PACK):
             mx(acc[t][:], wq[0], slice(t * P, (t + 1) * P), z0q, whole, True, False)
         z2_codes = held("z2_codes", [P, V], U32)
@@ -204,7 +207,7 @@ def tile_picked_zmix_relu_po_kernel(
         z2q = (z2_codes, z2_scales)
         z2b = []
         for a in range(HALVES):
-            tags = ["z0b", "late1", "late2"] if a == 0 else [None] * D
+            tags = ["far0_1", "far0_2", "far1_0", "far1_1", "far1_2", "far2_0"][D * a : D * (a + 1)]
             last = [gather("far3_%d_%d" % (d, a), 3, far_t[d], gate2_t, d, halves[a], tags[d]) for d in range(D)]
             turn_forward([(z2_fwd[a][0], slice(0, P))], 3, last)
             round_chunks(nc.scalar.copy, z2t[a], z2_fwd[a][0], 3, 4)
@@ -212,11 +215,11 @@ def tile_picked_zmix_relu_po_kernel(
             turn_back(z2t[a], back)
             z2b.append(held("z2b%d" % a, [P, P * PACK], BF16))
             nc.scalar.copy(z2b[a][:].bitcast(F32).rearrange("p (v u) -> p v u", u=2), back[:].rearrange("p u v -> p v u"))
-        wq[1] = quantize("w3q", wb[1][:], N, "z0b")
-        z1q = quantize("z1q", z1b[:], V, "late1")
+        wq[1] = quantize("w3q", wb[1][:], N, "far0_1")
+        z1q = quantize("z1q", z1b[:], V, "far0_2")
         for t in range(PACK):
             mx(acc[t][:], wq[1], slice(t * P, (t + 1) * P), z1q, whole, False, False)
-        wq[2] = quantize("w4q", wb[2][:], N, "late2")
+        wq[2] = quantize("w4q", wb[2][:], N, "far1_0")
         for a in range(HALVES):
             nc.vector.quantize_mx(out=z2_codes[:, halves[a]].bitcast(FP8X4), scales=z2_scales[:, halves[a]], in_=z2b[a][:])
 
@@ -236,7 +239,7 @@ def tile_picked_zmix_relu_po_kernel(
                 y[:].rearrange("p t (a i) -> p a t i", i=4)[:, quads],
             )
         y_codes, y_scales = quantize("yq", yb[:], V)
-        nc.sync.dma_start(out_1[0].rearrange("p n t -> p (n t)").bitcast(I32), y_codes[:].bitcast(I32))
         for q in range(4):
             eng = nc.scalar if q % 2 else nc.sync
             eng.dma_start(out_2[0, 4 * q : 4 * q + 4, :].bitcast(I32), y_scales[32 * q : 32 * q + 4, :].bitcast(I32))
+        nc.sync.dma_start(out_1[0].rearrange("p n t -> p (n t)").bitcast(I32), y_codes[:].bitcast(I32))

@@ -19,7 +19,12 @@ COPY = mybir.ActivationFunctionType.Copy
 
 P = 128
 PACK = 4
+GROUP = 16
+QUADRANTS = 4
+CHUNKS = H // P
 HALVES = V // P
+LINE = 4
+VECTOR_RUNS = 44
 
 
 def tile_picked_zmix_relu_po_kernel(
@@ -28,218 +33,239 @@ def tile_picked_zmix_relu_po_kernel(
     nc = tc.nc
     with ExitStack() as ctx:
         lists = ctx.enter_context(tc.tile_pool(name="lists", bufs=1))
-        sb = ctx.enter_context(tc.tile_pool(name="sb", bufs=1))
-        ps = ctx.enter_context(tc.psum_pool(name="ps", bufs=1))
+        sbuf = ctx.enter_context(tc.tile_pool(name="sbuf", bufs=1))
+        psum = ctx.enter_context(tc.psum_pool(name="psum", bufs=1))
 
-        def held(name, shape, dtype, tag=None):
-            return sb.tile(shape, dtype, name=name, tag=tag or name, align_bytes=64)
+        def held(name, shape, dtype, after=None):
+            return sbuf.tile(shape, dtype, name=name, tag=after or name, align_bytes=64)
 
-        def bank(name, b, shape):
-            return ps.tile(shape, F32, name=name, tag="bank%d" % b)
+        def bank(name, number, shape):
+            return psum.tile(shape, F32, name=name, tag="bank%d" % number)
 
         def load_list(name, src):
-            t = lists.tile(list(src.shape), U16, name=name)
-            nc.sync.dma_start(t[:], src)
-            return t
+            offsets = lists.tile(list(src.shape), U16, name=name)
+            nc.sync.dma_start(offsets[:], src)
+            return offsets
 
-        def load_w(name, w, c0, c1):
-            t = held(name, [P, PACK, c1 - c0], F32)
-            nc.sync.dma_start(t[:], w[:, c0:c1].rearrange("(p j) c -> p j c", j=PACK))
-            return t
+        def load_columns(name, w, first, stop):
+            raw = held(name, [P, PACK, stop - first], F32)
+            nc.sync.dma_start(raw[:], w[:, first:stop].rearrange("(p j) c -> p j c", j=PACK))
+            return raw
 
-        def load_gate(name, g, tag=None):
-            t = held(name, [P, D, V], F32, tag)
-            nc.sync.dma_start(t[:], g.rearrange("d p v -> p d v"))
-            return t
+        def load_gate(name, src, after=None):
+            weights = held(name, [P, D, V], F32, after)
+            nc.sync.dma_start(weights[:], src.rearrange("d p v -> p d v"))
+            return weights
 
-        def quantize(name, src, width, tag=None):
-            codes = held(name + "_codes", [P, width], U32, tag)
-            scales = held(name + "_scales", [P, width], U8)
-            nc.vector.quantize_mx(out=codes[:].bitcast(FP8X4), scales=scales[:], in_=src)
+        def quantize(codes, scales, rounded):
+            nc.vector.quantize_mx(out=codes.bitcast(FP8X4), scales=scales, in_=rounded)
             return codes, scales
 
-        def mx(out, stat, scols, mov, mcols, start, stop):
+        def quantize_new(name, rounded, width, after=None):
+            codes = held(name + "_codes", [P, width], U32, after)
+            scales = held(name + "_scales", [P, width], U8)
+            return quantize(codes[:], scales[:], rounded)
+
+        def product(out, stationary, moving, start, stop):
             nc.tensor.matmul_mx(
                 out=out,
-                lhsT=stat[0][:, scols].bitcast(FP8X4),
-                lhsT_scale=stat[1][:, scols],
-                rhs=mov[0][:, mcols].bitcast(FP8X4),
-                rhs_scale=mov[1][:, mcols],
+                lhsT=stationary[0].bitcast(FP8X4),
+                lhsT_scale=stationary[1],
+                rhs=moving[0].bitcast(FP8X4),
+                rhs_scale=moving[1],
                 start=start,
                 stop=stop,
             )
 
-        xs = held("xs", [P, T], U8)
-        nc.gpsimd.memset(xs[:].bitcast(I32), 0)
-        offs_t = load_list("offs_t", offs)
-        w1_raw = [load_w("w1r0", w1, 0, P)]
-        for q in range(4):
-            nc.sync.dma_start(xs[32 * q : 32 * q + 4, :].bitcast(I32), x_scales[0, 4 * q : 4 * q + 4, :].bitcast(I32))
-        xw = held("xw", [P, T], U32)
-        nc.sync.dma_start(xw[:].bitcast(I32), x_words[0].rearrange("p n t -> p (n t)").bitcast(I32))
-        w1_raw.append(load_w("w1r1", w1, P, 2 * P))
-        w1_rest = load_w("w1r2", w1, 2 * P, 4 * P)
-        cen_t = load_list("cen_t", cen)
-        gate_t = load_gate("gate_t", gate)
-        pos_t = [load_list("pos1_t", pos1)]
-        pos_t.append(load_list("pos2_t", pos2))
-        pos_t.append(load_list("pos3_t", pos3))
-        w2_raw = load_w("w2r", w2, 0, N)
-        w3_raw = load_w("w3r", w3, 0, N)
-        w4_raw = load_w("w4r", w4, 0, N)
-        far_t = [load_list("far1_t", far1), load_list("far2_t", far2), load_list("far3_t", far3)]
+        def columns(operand, cols):
+            return operand[0][:, cols], operand[1][:, cols]
+
+        x_scale_rows = held("x_scale_rows", [P, T], U8)
+        nc.gpsimd.memset(x_scale_rows[:].bitcast(I32), 0)
+        offs_list = load_list("offs_list", offs)
+        w1_first = load_columns("w1_first", w1, 0, P)
+        for q in range(QUADRANTS):
+            nc.sync.dma_start(
+                x_scale_rows[32 * q : 32 * q + 4, :].bitcast(I32), x_scales[0, 4 * q : 4 * q + 4, :].bitcast(I32)
+            )
+        x_codes = held("x_codes", [P, T], U32)
+        nc.sync.dma_start(x_codes[:].bitcast(I32), x_words[0].rearrange("p n t -> p (n t)").bitcast(I32))
+        w1_second = load_columns("w1_second", w1, P, 2 * P)
+        w1_rest = load_columns("w1_rest", w1, 2 * P, H)
+        cen_list = load_list("cen_list", cen)
+        near_gate = load_gate("near_gate", gate)
+        near_lists = [load_list("pos1_list", pos1), load_list("pos2_list", pos2), load_list("pos3_list", pos3)]
+        w2_raw = load_columns("w2_raw", w2, 0, N)
+        w3_raw = load_columns("w3_raw", w3, 0, N)
+        w4_raw = load_columns("w4_raw", w4, 0, N)
+        far_lists = [load_list("far1_list", far1), load_list("far2_list", far2), load_list("far3_list", far3)]
 
         ident = held("ident", [P, P], F32)
         make_identity(nc, ident[:])
 
-        w1_src = [w1_raw[0][:], w1_raw[1][:], w1_rest[:, :, 0:P], w1_rest[:, :, P : 2 * P]]
+        w1_raw = [w1_first[:], w1_second[:], w1_rest[:, :, 0:P], w1_rest[:, :, P : 2 * P]]
 
-        def w1_cast(c):
-            b = held("w1b%d" % c, [P, P * PACK], BF16)
+        def round_w1(c):
+            rounded = held("w1_rounded%d" % c, [P, P * PACK], BF16)
             nc.scalar.activation(
-                b[:].rearrange("p (a i j) -> p a j i", i=4, j=PACK),
-                w1_src[c].rearrange("p j (a i) -> p a j i", i=4),
+                rounded[:].rearrange("p (a i j) -> p a j i", i=LINE, j=PACK),
+                w1_raw[c].rearrange("p j (a i) -> p a j i", i=LINE),
                 COPY,
             )
-            return b
+            return rounded
 
-        xs_g = held("xs_g", [P, S], U8)
-        nc.vector.tensor_copy(xs_g[:], xs[:].indirect(offs_t[:]))
-        w1q = [quantize("w1q0", w1_cast(0)[:], P)]
-        xw_g = held("xw_g", [P, S], U32)
+        picked_scales = held("picked_scales", [P, S], U8)
+        nc.vector.tensor_copy(picked_scales[:], x_scale_rows[:].indirect(offs_list[:]))
+        w1_q = quantize_new("w1_q0", round_w1(0)[:], P)
+        picked_codes = held("picked_codes", [P, S], U32)
+        picked = (picked_codes[:], picked_scales[:])
+
+        list_halves = [slice(0, S // 2), slice(S // 2, S)]
+        for cols in list_halves:
+            offsets = offs_list[:, cols.start // GROUP : cols.stop // GROUP]
+            nc.vector.tensor_copy(picked_codes[:, cols], x_codes[:].indirect(offsets))
         h = [held("h0", [P, S], F32)]
-        for a in range(2):
-            nc.vector.tensor_copy(xw_g[:, a * 256 : (a + 1) * 256], xw[:].indirect(offs_t[:, 16 * a : 16 * (a + 1)]))
-        for a in range(2):
-            cols = slice(a * 256, (a + 1) * 256)
-            acc = bank("h0acc%d" % a, a, [P, 256])
-            mx(acc[:], w1q[0], slice(0, P), (xw_g, xs_g), cols, True, True)
+        for a, cols in enumerate(list_halves):
+            acc = bank("h0_acc%d" % a, a, [P, S // 2])
+            product(acc[:], w1_q, columns(picked, cols), True, True)
             nc.vector.tensor_scalar_max(h[0][:, cols], acc[:], 0.0)
 
-        w1b = [w1_cast(c) for c in range(1, 4)]
-        for c in range(1, 4):
-            w1q.append(quantize("w1q%d" % c, w1b[c - 1][:], P))
-            h.append(held("h%d" % c, [P, S], F32, "w1r2" if c == 1 else None))
-            acc = bank("hacc%d" % c, (c + 1) % 4, [P, S])
-            mx(acc[:], w1q[c], slice(0, P), (xw_g, xs_g), slice(0, S), True, True)
+        w1_rounded = [round_w1(c) for c in range(1, CHUNKS)]
+        for c, number in ((1, 2), (2, 3), (3, 0)):
+            w1_q = quantize_new("w1_q%d" % c, w1_rounded[c - 1][:], P)
+            h.append(held("h%d" % c, [P, S], F32, "w1_rest" if c == 1 else None))
+            acc = bank("h%d_acc" % c, number, [P, S])
+            product(acc[:], w1_q, picked, True, True)
             nc.scalar.activation(h[c][:], acc[:], RELU)
 
-        gate2_t = load_gate("gate2_t", gate2, "w1q3_codes")
+        far_gate = load_gate("far_gate", gate2, "w1_q3_codes")
 
-        def cast_w(name, raw, tag=None):
-            b = held(name, [P, N * PACK], BF16)
-            for c in range(2):
-                nc.scalar.copy(
-                    b[:].rearrange("p (t m j) -> p m j t", t=PACK, j=PACK)[:, 64 * c : 64 * (c + 1)],
-                    raw[:].rearrange("p j (m t) -> p m j t", t=PACK)[:, 64 * c : 64 * (c + 1)],
-                )
-            return b
+        def round_weights(name, raw, after=None):
+            rounded = held(name, [P, N * PACK], BF16, after)
+            dst = rounded[:].rearrange("p (t m j) -> p m j t", t=PACK, j=PACK)
+            src = raw[:].rearrange("p j (m t) -> p m j t", t=PACK)
+            for m in (slice(0, P // 2), slice(P // 2, P)):
+                nc.scalar.copy(dst[:, m], src[:, m])
+            return rounded
 
-        def turn_forward(fwd, c, terms):
+        def gather(out, c, offsets, weights=None):
+            if weights is None:
+                nc.vector.tensor_copy(out, h[c][:].indirect(offsets))
+            else:
+                nc.vector.tensor_tensor(out, h[c][:].indirect(offsets), weights, MULT)
+            return out
+
+        def gather_terms(name, c, term_lists, weights):
+            return [
+                gather(held("%s%d_%d" % (name, c, d), [P, V], F32)[:], c, term_lists[d][:], weights[:, d, :])
+                for d in range(D)
+            ]
+
+        def add_turned(sums, c, terms):
             for d, term in enumerate(terms):
-                for acc, cols in fwd:
+                for a, acc in enumerate(sums):
                     nc.tensor.matmul(
-                        acc[:, c * P : (c + 1) * P], term[:, cols], ident[:], start=(d == 0), stop=(d == len(terms) - 1), is_transpose=True
+                        acc[:, c * P : (c + 1) * P],
+                        term[:, a * P : (a + 1) * P],
+                        ident[:],
+                        start=(d == 0),
+                        stop=(d == len(terms) - 1),
+                        is_transpose=True,
                     )
 
-        def round_chunks(eng, zt, acc, c0, c1):
-            eng(
-                zt.rearrange("v (u p e) -> v u p e", u=2, e=2)[:, :, 32 * c0 : 32 * c1, :],
-                acc[:].rearrange("v (p u e) -> v u p e", u=2, e=2)[:, :, 32 * c0 : 32 * c1, :],
+        def round_pairs(pairs, acc, first, stop):
+            ps = slice(first * P // PACK, stop * P // PACK)
+            nc.scalar.copy(
+                pairs.rearrange("v (u p e) -> v u p e", u=2, e=2)[:, :, ps, :],
+                acc[:].rearrange("v (p u e) -> v u p e", u=2, e=2)[:, :, ps, :],
             )
 
-        def turn_back(zt, back):
+        def turn_back(back, pairs):
             for u in range(2):
-                nc.tensor.transpose(back[:, u, :], zt.bitcast(F32)[:, u * P : (u + 1) * P], ident[:])
+                nc.tensor.transpose(back[:, u, :], pairs.bitcast(F32)[:, u * P : (u + 1) * P], ident[:])
 
-        halves = [slice(a * P, (a + 1) * P) for a in range(HALVES)]
+        def interleave_pairs(rounded, back):
+            nc.scalar.copy(rounded.bitcast(F32).rearrange("p (v u) -> p v u", u=2), back[:].rearrange("p u v -> p v u"))
 
-        def gather(name, c, lst, g, d, cols, tag=None):
-            n = cols.stop - cols.start
-            t = held(name, [P, n], F32, tag)
-            win = h[c][:].indirect(lst[:, cols.start // 16 : cols.stop // 16])
-            if g is None:
-                nc.vector.tensor_copy(t[:], win)
-            else:
-                nc.vector.tensor_tensor(t[:], win, g[:, d, cols], MULT)
-            return t
+        def add_products(out_acc, weights, z, start, stop):
+            for t in range(PACK):
+                product(out_acc[t][:], columns(weights, slice(t * P, (t + 1) * P)), z, start, stop)
 
-        z0_fwd = [(bank("z0f%d" % a, 4 + a, [P, H]), halves[a]) for a in range(HALVES)]
-        z1_fwd = [(bank("z1f%d" % a, 6 + a, [P, H]), halves[a]) for a in range(HALVES)]
-        whole = slice(0, V)
-        wq = {}
-        for c in range(4):
-            turn_forward(z0_fwd, c, [gather("own%d" % c, c, cen_t, None, 0, whole)])
-            turn_forward(z1_fwd, c, [gather("near%d_%d" % (c, d), c, pos_t[d], gate_t, d, whole) for d in range(D)])
-        wb = [cast_w("w2b", w2_raw), cast_w("w3b", w3_raw), cast_w("w4b", w4_raw)]
+        z0_sums = [bank("z0_sums%d" % a, 4 + a, [P, H]) for a in range(HALVES)]
+        z1_sums = [bank("z1_sums%d" % a, 6 + a, [P, H]) for a in range(HALVES)]
+        for c in range(CHUNKS):
+            add_turned(z0_sums, c, [gather(held("own%d" % c, [P, V], F32)[:], c, cen_list[:])])
+            add_turned(z1_sums, c, gather_terms("near", c, near_lists, near_gate))
+        w2_rounded = round_weights("w2_rounded", w2_raw)
+        w3_rounded = round_weights("w3_rounded", w3_raw)
 
-        zt_all = held("zt_all", [P, 2 * HALVES * H], BF16, "w4r")
+        pairs01 = held("pairs01", [P, 2 * HALVES * H], BF16, "w3_raw")
 
-        def finish_z(name, fwd, backs, first):
+        def finish(name, sums, pairs, first_bank):
+            backs = [bank("%s_back%d" % (name, a), first_bank + a, [P, 2, P]) for a in range(HALVES)]
             for a in range(HALVES):
-                zt = zt_all[:, (first + a) * H : (first + a + 1) * H]
-                round_chunks(nc.scalar.copy, zt, fwd[a][0], 0, 4)
-                turn_back(zt, backs[a])
-            zb = held(name + "b", [P, V * PACK], BF16)
+                round_pairs(pairs[:, a * H : (a + 1) * H], sums[a], 0, CHUNKS)
+                turn_back(backs[a], pairs[:, a * H : (a + 1) * H])
+            rounded = held(name + "_rounded", [P, V * PACK], BF16)
             for a in range(HALVES):
-                nc.scalar.copy(
-                    zb[:].bitcast(F32).rearrange("p (a v u) -> p a v u", a=HALVES, u=2)[:, a],
-                    backs[a][:].rearrange("p u v -> p v u"),
-                )
-            return zb
+                interleave_pairs(rounded[:, a * H : (a + 1) * H], backs[a])
+            return rounded
 
-        z0b = finish_z("z0", z0_fwd, [bank("z0back%d" % a, 1 + a, [P, 2, P]) for a in range(HALVES)], 0)
-        z1b = finish_z("z1", z1_fwd, [bank("z1back%d" % a, 4 + a, [P, 2, P]) for a in range(HALVES)], HALVES)
+        z0_rounded = finish("z0", z0_sums, pairs01[:, 0 : HALVES * H], 1)
+        z1_rounded = finish("z1", z1_sums, pairs01[:, HALVES * H : 2 * HALVES * H], 4)
+        w4_rounded = round_weights("w4_rounded", w4_raw, "w3_raw")
 
-        z2_fwd = [(bank("z2f%d" % a, 4 + a, [P, H]), halves[a]) for a in range(HALVES)]
-        z2t = [held("z2t%d" % a, [P, H], BF16)[:] for a in range(HALVES)]
-        acc = [bank("out%d" % t, b, [P, V]) for t, b in enumerate((0, 3, 6, 7))]
-        for c in range(3):
-            turn_forward(z2_fwd, c, [gather("far%d_%d" % (c, d), c, far_t[d], gate2_t, d, whole) for d in range(D)])
+        z2_sums = [bank("z2_sums0", 7, [P, H]), bank("z2_sums1", 4, [P, H])]
+        z2_pairs = [held("z2_pairs%d" % a, [P, H], BF16)[:] for a in range(HALVES)]
+        last = CHUNKS - 1
+        for c in range(last):
+            add_turned(z2_sums, c, gather_terms("far", c, far_lists, far_gate))
         for a in range(HALVES):
-            round_chunks(nc.scalar.copy, z2t[a], z2_fwd[a][0], 0, 3)
-        wq[0] = quantize("w2q", wb[0][:], N)
-        z0q = quantize("z0q", z0b[:], V, "far0_0")
-        for t in range(PACK):
-            mx(acc[t][:], wq[0], slice(t * P, (t + 1) * P), z0q, whole, True, False)
-        z2_codes = held("z2_codes", [P, V], U32)
-        z2_scales = held("z2_scales", [P, V], U8)
-        z2q = (z2_codes, z2_scales)
-        z2b = []
+            round_pairs(z2_pairs[a], z2_sums[a], 0, last)
+
+        out_acc = [bank("out_acc%d" % t, number, [P, V]) for t, number in enumerate((0, 3, 5, 6))]
+        w2_q = quantize_new("w2_q", w2_rounded[:], N)
+        z0_q = quantize_new("z0_q", z0_rounded[:], V, "far0_0")
+        add_products(out_acc, w2_q, z0_q, True, False)
+
+        z2_rounded = []
         for a in range(HALVES):
-            tags = ["far0_1", "far0_2", "far1_0", "far1_1", "far1_2", "far2_0"][D * a : D * (a + 1)]
-            last = [gather("far3_%d_%d" % (d, a), 3, far_t[d], gate2_t, d, halves[a], tags[d]) for d in range(D)]
-            turn_forward([(z2_fwd[a][0], slice(0, P))], 3, last)
-            round_chunks(nc.scalar.copy, z2t[a], z2_fwd[a][0], 3, 4)
-            back = bank("z2back%d" % a, 1 + a, [P, 2, P])
-            turn_back(z2t[a], back)
-            z2b.append(held("z2b%d" % a, [P, P * PACK], BF16))
-            nc.scalar.copy(z2b[a][:].bitcast(F32).rearrange("p (v u) -> p v u", u=2), back[:].rearrange("p u v -> p v u"))
-        wq[1] = quantize("w3q", wb[1][:], N, "far0_1")
-        z1q = quantize("z1q", z1b[:], V, "far0_2")
-        for t in range(PACK):
-            mx(acc[t][:], wq[1], slice(t * P, (t + 1) * P), z1q, whole, False, False)
-        wq[2] = quantize("w4q", wb[2][:], N, "far1_0")
+            terms = held("far_last%d" % a, [P, D * P], F32, "far0_%d" % (a + 1))
+            targets = slice(a * P, (a + 1) * P)
+            for d in range(D):
+                offsets = far_lists[d][:, targets.start // GROUP : targets.stop // GROUP]
+                gather(terms[:, d * P : (d + 1) * P], last, offsets, far_gate[:, d, targets])
+            add_turned([z2_sums[a]], last, [terms[:, d * P : (d + 1) * P] for d in range(D)])
+            round_pairs(z2_pairs[a], z2_sums[a], last, CHUNKS)
+            back = bank("z2_back%d" % a, 1 + a, [P, 2, P])
+            turn_back(back, z2_pairs[a])
+            z2_rounded.append(held("z2_rounded%d" % a, [P, P * PACK], BF16))
+            interleave_pairs(z2_rounded[a][:], back)
+
+        late_codes = held("late_codes", [P, N + V + N], U32, "far0_1")
+        w3_q = quantize(late_codes[:, 0:N], held("w3_scales", [P, N], U8)[:], w3_rounded[:])
+        z1_q = quantize(late_codes[:, N : N + V], held("z1_scales", [P, V], U8)[:], z1_rounded[:])
+        add_products(out_acc, w3_q, z1_q, False, False)
+        w4_q = quantize(late_codes[:, N + V : N + V + N], held("w4_scales", [P, N], U8)[:], w4_rounded[:])
+        z2_q = (held("z2_codes", [P, V], U32)[:], held("z2_scales", [P, V], U8)[:])
         for a in range(HALVES):
-            nc.vector.quantize_mx(out=z2_codes[:, halves[a]].bitcast(FP8X4), scales=z2_scales[:, halves[a]], in_=z2b[a][:])
+            quantize(*columns(z2_q, slice(a * P, (a + 1) * P)), z2_rounded[a][:])
+        add_products(out_acc, w4_q, z2_q, False, True)
 
         y = held("y", [P, PACK, V], F32)
         out_rows = out_0.rearrange("(p t) v -> p t v", t=PACK)
-        for t in range(PACK):
-            mx(acc[t][:], wq[2], slice(t * P, (t + 1) * P), z2q, whole, False, True)
-            if t % 2 == 0:
-                nc.scalar.activation(y[:, t, :], acc[t][:], RELU)
-            else:
-                nc.vector.tensor_scalar_max(y[:, t, :], acc[t][:], 0.0)
-                nc.sync.dma_start(out_rows[:, t - 1 : t + 1, :], y[:, t - 1 : t + 1, :])
-        yb = held("yb", [P, V * PACK], BF16)
-        for eng, quads in ((nc.vector.tensor_copy, slice(0, 44)), (nc.scalar.copy, slice(44, 64))):
-            eng(
-                yb[:].rearrange("p (a i t) -> p a t i", i=4, t=PACK)[:, quads],
-                y[:].rearrange("p t (a i) -> p a t i", i=4)[:, quads],
-            )
-        y_codes, y_scales = quantize("yq", yb[:], V)
-        for q in range(4):
-            eng = nc.scalar if q % 2 else nc.sync
-            eng.dma_start(out_2[0, 4 * q : 4 * q + 4, :].bitcast(I32), y_scales[32 * q : 32 * q + 4, :].bitcast(I32))
-        nc.sync.dma_start(out_1[0].rearrange("p n t -> p (n t)").bitcast(I32), y_codes[:].bitcast(I32))
+        for t in range(0, PACK, 2):
+            nc.scalar.activation(y[:, t, :], out_acc[t][:], RELU)
+            nc.vector.tensor_scalar_max(y[:, t + 1, :], out_acc[t + 1][:], 0.0)
+            nc.sync.dma_start(out_rows[:, t : t + 2, :], y[:, t : t + 2, :])
+        y_rounded = held("y_rounded", [P, V * PACK], BF16)
+        dst = y_rounded[:].rearrange("p (a i t) -> p a t i", i=LINE, t=PACK)
+        src = y[:].rearrange("p t (a i) -> p a t i", i=LINE)
+        nc.vector.tensor_copy(dst[:, :VECTOR_RUNS], src[:, :VECTOR_RUNS])
+        nc.scalar.copy(dst[:, VECTOR_RUNS:], src[:, VECTOR_RUNS:])
+        y_codes, y_scales = quantize_new("y_q", y_rounded[:], V)
+
+        nc.sync.dma_start(out_1[0].rearrange("p n t -> p (n t)").bitcast(I32), y_codes.bitcast(I32))
+        for q in range(QUADRANTS):
+            queue = nc.sync if q == QUADRANTS - 1 else nc.scalar
+            queue.dma_start(out_2[0, 4 * q : 4 * q + 4, :].bitcast(I32), y_scales[32 * q : 32 * q + 4, :].bitcast(I32))

from contextlib import ExitStack

import concourse.mybir as mybir
from concourse.masks import make_identity

K, T, S, D, V, H, N = 512, 1024, 512, 3, 256, 512, 512
FLOPS = 2 * K * H * S + 3 * 2 * H * N * V

F32 = mybir.dt.float32
BF16 = mybir.dt.bfloat16
I32 = mybir.dt.int32
U32 = mybir.dt.uint32
U16 = mybir.dt.uint16
U8 = mybir.dt.uint8
FP8X4 = mybir.dt.float8_e4m3fn_x4
MULT = mybir.AluOpType.mult
RELU = mybir.ActivationFunctionType.Relu
COPY = mybir.ActivationFunctionType.Copy

P = 128
PACK = 4
GROUP = 16
QUADRANTS = 4
CHUNKS = H // P
HALVES = V // P
LINE = 4
VECTOR_RUNS = 44


def tile_picked_zmix_relu_po_kernel(
    tc, x_words, x_scales, w1, w2, w3, w4, gate, gate2, offs, cen, pos1, pos2, pos3, far1, far2, far3, out_0, out_1, out_2
):
    nc = tc.nc
    with ExitStack() as ctx:
        lists = ctx.enter_context(tc.tile_pool(name="lists", bufs=1))
        sbuf = ctx.enter_context(tc.tile_pool(name="sbuf", bufs=1))
        psum = ctx.enter_context(tc.psum_pool(name="psum", bufs=1))

        def held(name, shape, dtype, after=None):
            return sbuf.tile(shape, dtype, name=name, tag=after or name, align_bytes=64)

        def bank(name, number, shape):
            return psum.tile(shape, F32, name=name, tag="bank%d" % number)

        def load_list(name, src):
            offsets = lists.tile(list(src.shape), U16, name=name)
            nc.sync.dma_start(offsets[:], src)
            return offsets

        def load_columns(name, w, first, stop):
            raw = held(name, [P, PACK, stop - first], F32)
            nc.sync.dma_start(raw[:], w[:, first:stop].rearrange("(p j) c -> p j c", j=PACK))
            return raw

        def load_gate(name, src, after=None):
            weights = held(name, [P, D, V], F32, after)
            nc.sync.dma_start(weights[:], src.rearrange("d p v -> p d v"))
            return weights

        def quantize(codes, scales, rounded):
            nc.vector.quantize_mx(out=codes.bitcast(FP8X4), scales=scales, in_=rounded)
            return codes, scales

        def quantize_new(name, rounded, width, after=None):
            codes = held(name + "_codes", [P, width], U32, after)
            scales = held(name + "_scales", [P, width], U8)
            return quantize(codes[:], scales[:], rounded)

        def product(out, stationary, moving, start, stop):
            nc.tensor.matmul_mx(
                out=out,
                lhsT=stationary[0].bitcast(FP8X4),
                lhsT_scale=stationary[1],
                rhs=moving[0].bitcast(FP8X4),
                rhs_scale=moving[1],
                start=start,
                stop=stop,
            )

        def columns(operand, cols):
            return operand[0][:, cols], operand[1][:, cols]

        x_scale_rows = held("x_scale_rows", [P, T], U8)
        nc.gpsimd.memset(x_scale_rows[:].bitcast(I32), 0)
        offs_list = load_list("offs_list", offs)
        w1_first = load_columns("w1_first", w1, 0, P)
        for q in range(QUADRANTS):
            nc.sync.dma_start(
                x_scale_rows[32 * q : 32 * q + 4, :].bitcast(I32), x_scales[0, 4 * q : 4 * q + 4, :].bitcast(I32)
            )
        x_codes = held("x_codes", [P, T], U32)
        nc.sync.dma_start(x_codes[:].bitcast(I32), x_words[0].rearrange("p n t -> p (n t)").bitcast(I32))
        w1_second = load_columns("w1_second", w1, P, 2 * P)
        w1_rest = load_columns("w1_rest", w1, 2 * P, H)
        cen_list = load_list("cen_list", cen)
        near_gate = load_gate("near_gate", gate)
        near_lists = [load_list("pos1_list", pos1), load_list("pos2_list", pos2), load_list("pos3_list", pos3)]
        w2_raw = load_columns("w2_raw", w2, 0, N)
        w3_raw = load_columns("w3_raw", w3, 0, N)
        w4_raw = load_columns("w4_raw", w4, 0, N)
        far_lists = [load_list("far1_list", far1), load_list("far2_list", far2), load_list("far3_list", far3)]

        ident = held("ident", [P, P], F32)
        make_identity(nc, ident[:])

        w1_raw = [w1_first[:], w1_second[:], w1_rest[:, :, 0:P], w1_rest[:, :, P : 2 * P]]

        def round_w1(c):
            rounded = held("w1_rounded%d" % c, [P, P * PACK], BF16)
            nc.scalar.activation(
                rounded[:].rearrange("p (a i j) -> p a j i", i=LINE, j=PACK),
                w1_raw[c].rearrange("p j (a i) -> p a j i", i=LINE),
                COPY,
            )
            return rounded

        picked_scales = held("picked_scales", [P, S], U8)
        nc.vector.tensor_copy(picked_scales[:], x_scale_rows[:].indirect(offs_list[:]))
        w1_q = quantize_new("w1_q0", round_w1(0)[:], P)
        picked_codes = held("picked_codes", [P, S], U32)
        picked = (picked_codes[:], picked_scales[:])

        list_halves = [slice(0, S // 2), slice(S // 2, S)]
        for cols in list_halves:
            offsets = offs_list[:, cols.start // GROUP : cols.stop // GROUP]
            nc.vector.tensor_copy(picked_codes[:, cols], x_codes[:].indirect(offsets))
        h = [held("h0", [P, S], F32)]
        for a, cols in enumerate(list_halves):
            acc = bank("h0_acc%d" % a, a, [P, S // 2])
            product(acc[:], w1_q, columns(picked, cols), True, True)
            nc.vector.tensor_scalar_max(h[0][:, cols], acc[:], 0.0)

        w1_rounded = [round_w1(c) for c in range(1, CHUNKS)]
        for c, number in ((1, 2), (2, 3), (3, 0)):
            w1_q = quantize_new("w1_q%d" % c, w1_rounded[c - 1][:], P)
            h.append(held("h%d" % c, [P, S], F32, "w1_rest" if c == 1 else None))
            acc = bank("h%d_acc" % c, number, [P, S])
            product(acc[:], w1_q, picked, True, True)
            nc.scalar.activation(h[c][:], acc[:], RELU)

        far_gate = load_gate("far_gate", gate2, "w1_q3_codes")

        def round_weights(name, raw, after=None):
            rounded = held(name, [P, N * PACK], BF16, after)
            dst = rounded[:].rearrange("p (t m j) -> p m j t", t=PACK, j=PACK)
            src = raw[:].rearrange("p j (m t) -> p m j t", t=PACK)
            for m in (slice(0, P // 2), slice(P // 2, P)):
                nc.scalar.copy(dst[:, m], src[:, m])
            return rounded

        def gather(out, c, offsets, weights=None):
            if weights is None:
                nc.vector.tensor_copy(out, h[c][:].indirect(offsets))
            else:
                nc.vector.tensor_tensor(out, h[c][:].indirect(offsets), weights, MULT)
            return out

        def gather_terms(name, c, term_lists, weights):
            return [
                gather(held("%s%d_%d" % (name, c, d), [P, V], F32)[:], c, term_lists[d][:], weights[:, d, :])
                for d in range(D)
            ]

        def add_turned(sums, c, terms):
            for d, term in enumerate(terms):
                for a, acc in enumerate(sums):
                    nc.tensor.matmul(
                        acc[:, c * P : (c + 1) * P],
                        term[:, a * P : (a + 1) * P],
                        ident[:],
                        start=(d == 0),
                        stop=(d == len(terms) - 1),
                        is_transpose=True,
                    )

        def round_pairs(pairs, acc, first, stop):
            ps = slice(first * P // PACK, stop * P // PACK)
            nc.scalar.copy(
                pairs.rearrange("v (u p e) -> v u p e", u=2, e=2)[:, :, ps, :],
                acc[:].rearrange("v (p u e) -> v u p e", u=2, e=2)[:, :, ps, :],
            )

        def turn_back(back, pairs):
            for u in range(2):
                nc.tensor.transpose(back[:, u, :], pairs.bitcast(F32)[:, u * P : (u + 1) * P], ident[:])

        def interleave_pairs(rounded, back):
            nc.scalar.copy(rounded.bitcast(F32).rearrange("p (v u) -> p v u", u=2), back[:].rearrange("p u v -> p v u"))

        def add_products(out_acc, weights, z, start, stop):
            for t in range(PACK):
                product(out_acc[t][:], columns(weights, slice(t * P, (t + 1) * P)), z, start, stop)

        z0_sums = [bank("z0_sums%d" % a, 4 + a, [P, H]) for a in range(HALVES)]
        z1_sums = [bank("z1_sums%d" % a, 6 + a, [P, H]) for a in range(HALVES)]
        for c in range(CHUNKS):
            add_turned(z0_sums, c, [gather(held("own%d" % c, [P, V], F32)[:], c, cen_list[:])])
            add_turned(z1_sums, c, gather_terms("near", c, near_lists, near_gate))
        w2_rounded = round_weights("w2_rounded", w2_raw)
        w3_rounded = round_weights("w3_rounded", w3_raw)

        pairs01 = held("pairs01", [P, 2 * HALVES * H], BF16, "w3_raw")

        def finish(name, sums, pairs, first_bank):
            backs = [bank("%s_back%d" % (name, a), first_bank + a, [P, 2, P]) for a in range(HALVES)]
            for a in range(HALVES):
                round_pairs(pairs[:, a * H : (a + 1) * H], sums[a], 0, CHUNKS)
                turn_back(backs[a], pairs[:, a * H : (a + 1) * H])
            rounded = held(name + "_rounded", [P, V * PACK], BF16)
            for a in range(HALVES):
                interleave_pairs(rounded[:, a * H : (a + 1) * H], backs[a])
            return rounded

        z0_rounded = finish("z0", z0_sums, pairs01[:, 0 : HALVES * H], 1)
        z1_rounded = finish("z1", z1_sums, pairs01[:, HALVES * H : 2 * HALVES * H], 4)
        w4_rounded = round_weights("w4_rounded", w4_raw, "w3_raw")

        z2_sums = [bank("z2_sums0", 7, [P, H]), bank("z2_sums1", 4, [P, H])]
        z2_pairs = [held("z2_pairs%d" % a, [P, H], BF16)[:] for a in range(HALVES)]
        last = CHUNKS - 1
        for c in range(last):
            add_turned(z2_sums, c, gather_terms("far", c, far_lists, far_gate))
        for a in range(HALVES):
            round_pairs(z2_pairs[a], z2_sums[a], 0, last)

        out_acc = [bank("out_acc%d" % t, number, [P, V]) for t, number in enumerate((0, 3, 5, 6))]
        w2_q = quantize_new("w2_q", w2_rounded[:], N)
        z0_q = quantize_new("z0_q", z0_rounded[:], V, "far0_0")
        add_products(out_acc, w2_q, z0_q, True, False)

        z2_rounded = []
        for a in range(HALVES):
            terms = held("far_last%d" % a, [P, D * P], F32, "far0_%d" % (a + 1))
            targets = slice(a * P, (a + 1) * P)
            for d in range(D):
                offsets = far_lists[d][:, targets.start // GROUP : targets.stop // GROUP]
                gather(terms[:, d * P : (d + 1) * P], last, offsets, far_gate[:, d, targets])
            add_turned([z2_sums[a]], last, [terms[:, d * P : (d + 1) * P] for d in range(D)])
            round_pairs(z2_pairs[a], z2_sums[a], last, CHUNKS)
            back = bank("z2_back%d" % a, 1 + a, [P, 2, P])
            turn_back(back, z2_pairs[a])
            z2_rounded.append(held("z2_rounded%d" % a, [P, P * PACK], BF16))
            interleave_pairs(z2_rounded[a][:], back)

        late_codes = held("late_codes", [P, N + V + N], U32, "far0_1")
        w3_q = quantize(late_codes[:, 0:N], held("w3_scales", [P, N], U8)[:], w3_rounded[:])
        z1_q = quantize(late_codes[:, N : N + V], held("z1_scales", [P, V], U8)[:], z1_rounded[:])
        add_products(out_acc, w3_q, z1_q, False, False)
        w4_q = quantize(late_codes[:, N + V : N + V + N], held("w4_scales", [P, N], U8)[:], w4_rounded[:])
        z2_q = (held("z2_codes", [P, V], U32)[:], held("z2_scales", [P, V], U8)[:])
        for a in range(HALVES):
            quantize(*columns(z2_q, slice(a * P, (a + 1) * P)), z2_rounded[a][:])
        add_products(out_acc, w4_q, z2_q, False, True)

        y = held("y", [P, PACK, V], F32)
        out_rows = out_0.rearrange("(p t) v -> p t v", t=PACK)
        for t in range(0, PACK, 2):
            nc.scalar.activation(y[:, t, :], out_acc[t][:], RELU)
            nc.vector.tensor_scalar_max(y[:, t + 1, :], out_acc[t + 1][:], 0.0)
            nc.sync.dma_start(out_rows[:, t : t + 2, :], y[:, t : t + 2, :])
        y_rounded = held("y_rounded", [P, V * PACK], BF16)
        dst = y_rounded[:].rearrange("p (a i t) -> p a t i", i=LINE, t=PACK)
        src = y[:].rearrange("p t (a i) -> p a t i", i=LINE)
        nc.vector.tensor_copy(dst[:, :VECTOR_RUNS], src[:, :VECTOR_RUNS])
        nc.scalar.copy(dst[:, VECTOR_RUNS:], src[:, VECTOR_RUNS:])
        y_codes, y_scales = quantize_new("y_q", y_rounded[:], V)

        nc.sync.dma_start(out_1[0].rearrange("p n t -> p (n t)").bitcast(I32), y_codes.bitcast(I32))
        for q in range(QUADRANTS):
            queue = nc.sync if q == QUADRANTS - 1 else nc.scalar
            queue.dma_start(out_2[0, 4 * q : 4 * q + 4, :].bitcast(I32), y_scales[32 * q : 32 * q + 4, :].bitcast(I32))
